import numpy as np
import ml_dtypes


def mxq(x, axis, fmt="e4m3"):
    dtype, down = {"e4m3": (ml_dtypes.float8_e4m3fn, 7), "e5m2": (ml_dtypes.float8_e5m2, 14)}[fmt]
    v = np.moveaxis(np.asarray(x, np.float32).astype(ml_dtypes.bfloat16).astype(np.float64), axis, -1)
    blocks = v.reshape(v.shape[:-1] + (-1, 32))
    amax = np.abs(blocks).max(-1, keepdims=True)
    byte = np.maximum(np.where(amax > 0, np.frexp(amax)[1] - 1 + 127, 0) - down, 1)
    scale = np.exp2(byte - 127.0)
    codes = (blocks / scale).astype(np.float32).astype(dtype).astype(np.float64)
    return np.moveaxis((codes * scale).reshape(v.shape), -1, axis)


WIDE = False


def mx_kscale(k):
    if not WIDE:
        return np.ones(k)
    levels = np.array([10, -10, 5, -5, 0])
    if k % 512:
        return np.exp2(np.random.permutation(np.resize(levels, k // 32))).repeat(32)
    a = np.empty((k // 512, 16))
    for p in range(k // 512):
        a[p, :8] = np.random.permutation(np.resize(levels, 8))
        for g in range(8):
            far = levels[np.abs(levels - a[p, g]) >= 10]
            a[p, g + 8] = far[np.random.randint(len(far))]
    return np.exp2(a.ravel()).repeat(32)


def f64(x):
    return np.asarray(x).astype(np.float64)


def striped(idx):
    return np.tile(idx.reshape(-1, 16).T, (8, 1)).astype(np.uint16)


def unstriped(offs):
    return offs[:16].T.reshape(-1).astype(np.int64)


def striped8(idx):
    return np.concatenate([x.reshape(-1, 16).T for x in idx]).astype(np.uint16)


def runs(offs, k):
    lists = np.stack([offs[16 * r : 16 * r + 16].T.reshape(-1) for r in range(8)]).astype(np.int64)
    return lists[np.arange(k) % 512 // 64]


def pack_weight(w):
    k, n = w.shape
    w = f64(np.asarray(w, np.float32).astype(ml_dtypes.bfloat16)).reshape(k // 32, 32, n)
    amax = np.abs(w).max(1)
    byte = np.clip(np.where(amax > 0, np.frexp(amax)[1] - 1 + 127 - 7, 1), 1, 254)
    scaled = (w * np.exp2(127.0 - byte)[:, None, :]).reshape(k, n).astype(np.float32)
    words = np.ascontiguousarray(scaled.reshape(k // 512, 128, 4, n).transpose(0, 1, 3, 2)).astype(ml_dtypes.float8_e4m3fn).view(np.uint8)
    return words, np.ascontiguousarray(byte.astype(np.uint8).reshape(k // 512, 16, n))


def unpack_weight(words, scales):
    g, p, n, _ = words.shape
    vals = np.ascontiguousarray(words).view(ml_dtypes.float8_e4m3fn).astype(np.float64) * np.repeat(np.exp2(scales.astype(np.float64) - 127.0), 8, axis=1)[..., None]
    return vals.transpose(0, 1, 3, 2).reshape(g * 512, n)


def sigmoid(v):
    return 1.0 / (1.0 + np.exp(-np.maximum(v, -700.0)))


K, T, S, V, N, H = 512, 2048, 512, 512, 512, 512


def setup_inputs():
    n = np.random.standard_normal
    s = mx_kscale(K)[:, None]
    u = mx_kscale(H)
    packed_xT = pack_weight(n((K, T)) * s)
    return {
        "x_words": packed_xT[0],
        "x_scales": packed_xT[1],
        "w1": (n((K, H)) / np.sqrt(K) / s * u).astype(np.float32),
        "a1": np.repeat(np.random.uniform(0.1, 0.6, (8, V)), 64, axis=0).astype(np.float32),
        "a2": np.repeat(np.random.uniform(0.1, 0.6, (8, V)), 64, axis=0).astype(np.float32),
        "a3": np.repeat(np.random.uniform(0.1, 0.6, (8, V)), 64, axis=0).astype(np.float32),
        "w2": (n((H, N)) / np.sqrt(H) / u[:, None]).astype(np.float32),
        "w3": (n((K, N)) / np.sqrt(K) / s).astype(np.float32),
        "offs": striped(np.random.permutation(T)[:S]),
        "p1": striped8(np.stack([np.random.permutation(S) for _ in range(8)])),
        "p2": striped8(np.stack([np.random.permutation(S) for _ in range(8)])),
        "p3": striped8(np.stack([np.random.permutation(S) for _ in range(8)])),
        "own": striped(np.random.permutation(T)[:V]),
    }


def reference(x_words, x_scales, w1, a1, a2, a3, w2, w3, offs, p1, p2, p3, own):
    xq = unpack_weight(x_words, x_scales)[:, unstriped(offs)]
    y = mxq(f64(w1), 0, "e4m3").T @ xq
    z = (y[np.arange(H)[:, None], runs(p1, H)]) * f64(a1) + (y[np.arange(H)[:, None], runs(p2, H)]) * f64(a2) + (y[np.arange(H)[:, None], runs(p3, H)]) * f64(a3)
    o = mxq(f64(w2), 0, "e4m3").T @ mxq(z, 0, "e4m3")
    x_own = unpack_weight(x_words, x_scales)[:, unstriped(own)]
    s = sigmoid(mxq(f64(w3), 0, "e4m3").T @ x_own)
    return o * s

@@ -1,0 +1,183 @@
+from contextlib import ExitStack
+
+import concourse.mybir as mybir
+from concourse.masks import make_identity
+
+K, T, S, V, H, N = 512, 2048, 512, 512, 512, 512
+FLOPS = 2 * K * H * S + 2 * H * N * V + 2 * K * N * V
+BYTES = K * T + 16 * T + 4 * (K * H + H * N + K * N) + 3 * 4 * 8 * V + 5 * 2 * 128 * 32 + 4 * N * V
+
+F32 = mybir.dt.float32
+BF16 = mybir.dt.bfloat16
+I32 = mybir.dt.int32
+U32 = mybir.dt.uint32
+U16 = mybir.dt.uint16
+U8 = mybir.dt.uint8
+FP8X4 = mybir.dt.float8_e4m3fn_x4
+MULT = mybir.AluOpType.mult
+SIGMOID = mybir.ActivationFunctionType.Sigmoid
+
+P = 128
+PACK = 4
+GROUP = 16
+BLK = 128
+
+
+def tile_picked_gatehead_none_p_kernel(tc, x_words, x_scales, w1, a1, a2, a3, w2, w3, offs, p1, p2, p3, own, out):
+    nc = tc.nc
+    with ExitStack() as ctx:
+        keep = ctx.enter_context(tc.tile_pool(name="keep", bufs=1))
+        psum = ctx.enter_context(tc.psum_pool(name="psum", bufs=1))
+
+        def sb(name, shape, dtype, tag=None):
+            return keep.tile(shape, dtype, name=name, tag=tag or name, align_bytes=64)
+
+        def bank(tag, name, shape):
+            return psum.tile(shape, F32, name=name, tag=tag)
+
+        def load_list(name, src):
+            t = keep.tile([P, S // GROUP], U16, name=name)
+            nc.sync.dma_start(t[:], src)
+            return t
+
+        offs_t = load_list("offs_t", offs)
+        xs_in = sb("xs_in", [P, T], U8)
+        for q in range(4):
+            nc.scalar.dma_start(xs_in[32 * q : 32 * q + 4, :].bitcast(I32), x_scales[0, 4 * q : 4 * q + 4, :].bitcast(I32))
+        w1_rows = w1.rearrange("(p j) c -> p j c", j=PACK)
+        w1_raw = []
+        for h in range(2):
+            t = sb("w1_raw%d" % h, [P, PACK, H // 2], F32)
+            nc.sync.dma_start(t[:], w1_rows[:, :, h * (H // 2) : (h + 1) * (H // 2)])
+            w1_raw.append(t)
+        own_t = load_list("own_t", own)
+        xw = sb("xw", [P, T], U32)
+        nc.sync.dma_start(xw[:].bitcast(I32), x_words[0].rearrange("p n j -> p (n j)").bitcast(I32))
+        lists, gains = [], []
+        for l, (p_l, a_l) in enumerate(((p1, a1), (p2, a2), (p3, a3))):
+            lists.append(load_list("p%d_t" % l, p_l))
+            g = sb("a%d_t" % l, [P, V], F32)
+            nc.sync.dma_start(g[:], a_l.rearrange("(p j) v -> p j v", j=PACK)[:, 0, :])
+            gains.append(g)
+        w3_raw = sb("w3_raw", [P, PACK, N], F32)
+        nc.sync.dma_start(w3_raw[:], w3.rearrange("(p j) c -> p j c", j=PACK))
+        w2_raw = sb("w2_raw", [P, PACK, N], F32)
+        nc.sync.dma_start(w2_raw[:], w2.rearrange("(p j) c -> p j c", j=PACK))
+
+        ident = sb("ident", [P, P], F32)
+        make_identity(nc, ident[:])
+
+        def pick(name, table, lst, dtype):
+            t = sb(name, [P, S], dtype)
+            nc.vector.tensor_copy(t[:], table[:].indirect(lst[:]))
+            return t
+
+        xs = sb("xs", [P, T], U8)
+        nc.vector.memset(xs[:].bitcast(I32), 0)
+        for q in range(4):
+            nc.vector.tensor_copy(xs[32 * q : 32 * q + 4, :].bitcast(I32), xs_in[32 * q : 32 * q + 4, :].bitcast(I32))
+        xq_s = pick("xq_s", xs, offs_t, U8)
+
+        def quantize(name, grouped, width):
+            codes = sb(name + "_codes", [P, width], U32)
+            scales = sb(name + "_scales", [P, width], U8)
+            nc.vector.quantize_mx(out=codes[:].bitcast(FP8X4), scales=scales[:], in_=grouped)
+            return codes, scales
+
+        def mx(out_ap, w_q, cols, x_codes, x_scale):
+            nc.tensor.matmul_mx(out=out_ap, lhsT=w_q[0][:, cols].bitcast(FP8X4), lhsT_scale=w_q[1][:, cols],
+                                rhs=x_codes.bitcast(FP8X4), rhs_scale=x_scale, start=True, stop=True)
+
+        w1_b = sb("w1_b", [P, PACK, P, PACK], BF16)
+        for h in range(2):
+            nc.scalar.copy(w1_b[:, :, 64 * h : 64 * (h + 1), :].rearrange("p t m j -> p m j t"),
+                 w1_raw[h][:].rearrange("p j (m t) -> p m j t", t=PACK))
+        w1_q = quantize("w1", w1_b[:].rearrange("p t m j -> p (t m j)"), H)
+        xq_w = pick("xq_w", xw, offs_t, U32)
+        xo_s = pick("xo_s", xs, own_t, U8)
+        xo_w = pick("xo_w", xw, own_t, U32)
+        y = []
+        for t in range(PACK):
+            acc = bank("A%d" % t, "y_ps%d" % t, [P, S])
+            mx(acc[:], w1_q, slice(P * t, P * (t + 1)), xq_w[:], xq_s[:])
+            y_t = sb("y%d" % t, [P, S], F32)
+            nc.scalar.copy(y_t[:], acc[:])
+            y.append(y_t)
+
+        def round_weights(name, raw):
+            grouped = sb(name, [P, N, PACK], BF16)
+            nc.scalar.copy(grouped[:].rearrange("p (c i) j -> p c j i", i=4), raw[:].rearrange("p j (c i) -> p c j i", i=4))
+            return grouped[:].rearrange("p c j -> p (c j)")
+
+        w3_q = quantize("w3", round_weights("w3_b", w3_raw), N)
+        w2_b = round_weights("w2_b", w2_raw)
+        w2_q = quantize("w2", w2_b, N)
+
+        gate = sb("gate", [P, PACK, V], F32)
+
+        def make_gate():
+            for mt in range(PACK):
+                acc = bank("A%d" % mt, "g_ps%d" % mt, [P, V])
+                mx(acc[:], w3_q, slice(P * mt, P * (mt + 1)), xo_w[:], xo_s[:])
+                nc.scalar.activation(gate[:, mt, :], acc[:], SIGMOID)
+
+        out_rows = out.rearrange("(mt p) v -> p mt v", p=P)
+
+        def gather_sum(blocks, prods, after_pair=None):
+            v0, v1 = blocks[0] * BLK, (blocks[-1] + 1) * BLK
+            z_t = [bank("B%d" % b, "zT%d" % b, [P, PACK, P]) for b in blocks]
+            for t in range(PACK):
+                for l in range(3):
+                    prod = prods(t)[:, l, :]
+                    nc.vector.tensor_tensor(prod, y[t][:].indirect(lists[l][:, v0 // GROUP : v1 // GROUP]), gains[l][:, v0:v1], MULT)
+                    for i in range(len(blocks)):
+                        nc.tensor.matmul(z_t[i][:, t, :], lhsT=prod[:, i * BLK : (i + 1) * BLK], rhs=ident[:],
+                                         is_transpose=True, start=(l == 0), stop=(l == 2))
+                if after_pair is not None and t % 2 == 1:
+                    after_pair(t // 2, z_t[0])
+            return z_t
+
+        def project(b, zb):
+            back = bank("A%d" % b, "back%d" % b, [P, 2, BLK])
+            for u in range(2):
+                nc.tensor.transpose(back[:, u, :], zb[u].rearrange("v p e -> v (p e)").bitcast(F32), ident[:])
+            zq = sb("zq%d" % b, [P, BLK * PACK], BF16)
+            nc.scalar.copy(zq[:].bitcast(F32).rearrange("p (v u) -> p v u", u=2), back[:].rearrange("p u v -> p v u"))
+            z_q = quantize("z%d" % b, zq[:], BLK)
+            acc = bank("A%d" % b, "o_ps%d" % b, [P, PACK, BLK])
+            for mt in range(PACK):
+                mx(acc[:, mt, :], w2_q, slice(P * mt, P * (mt + 1)), z_q[0][:], z_q[1][:])
+            return acc
+
+        def finish(b, acc, tag=None):
+            res = sb("res%d" % b, [P, PACK, BLK], F32, tag)
+            nc.vector.tensor_tensor(res[:], acc[:], gate[:, :, b * BLK : (b + 1) * BLK], MULT)
+            nc.sync.dma_start(out_rows[:, :, b * BLK : (b + 1) * BLK], res[:])
+
+        make_gate()
+        made = {}
+
+        def first_prods(t):
+            if t not in made:
+                made[t] = sb("g%d" % t, [P, 3, 3 * BLK], F32, {2: "w3_b", 3: "w2_b"}.get(t))
+            return made[t]
+
+        projected = []
+        for b, z_b in enumerate(gather_sum([0, 1, 2], first_prods)):
+            zb = sb("zb%d" % b, [P, 2, P, 2], BF16)
+            nc.scalar.copy(zb[:], z_b[:].rearrange("v (u e) p -> v u p e", e=2))
+            projected.append(project(b, [zb[:, u, :, :] for u in range(2)]))
+
+        c01 = sb("c01", [P, 2, 3, BLK], F32, "w3_b")
+        c2 = sb("c2", [P, 3, BLK], F32, "zq0")
+        c3 = sb("c3", [P, 3, BLK], F32, "zq1")
+        last_prods = [c01[:, 0, :, :], c01[:, 1, :, :], c2[:], c3[:]]
+        halves = [sb("zb3_%d" % u, [P, P, 2], BF16) for u in range(2)]
+
+        def round_pair(u, z_b):
+            nc.scalar.copy(halves[u][:], z_b[:, 2 * u : 2 * u + 2, :].rearrange("v e p -> v p e"))
+
+        gather_sum([3], lambda t: last_prods[t], round_pair)
+        projected.append(project(3, [h[:] for h in halves]))
+        for b in range(V // BLK):
+            finish(b, projected[b], "zq0" if b == 0 else None)

@@ -21,6 +21,7 @@ P = 128
 PACK = 4
 GROUP = 16
 BLK = 128
+HALF = 256
 
 
 def tile_picked_gatehead_none_p_kernel(tc, x_words, x_scales, w1, a1, a2, a3, w2, w3, offs, p1, p2, p3, own, out):
@@ -43,7 +44,7 @@ def tile_picked_gatehead_none_p_kernel(tc, x_words, x_scales, w1, a1, a2, a3, w2
         offs_t = load_list("offs_t", offs)
         xs_in = sb("xs_in", [P, T], U8)
         for q in range(4):
-            nc.scalar.dma_start(xs_in[32 * q : 32 * q + 4, :].bitcast(I32), x_scales[0, 4 * q : 4 * q + 4, :].bitcast(I32))
+            nc.sync.dma_start(xs_in[32 * q : 32 * q + 4, :].bitcast(I32), x_scales[0, 4 * q : 4 * q + 4, :].bitcast(I32))
         w1_rows = w1.rearrange("(p j) c -> p j c", j=PACK)
         w1_raw = []
         for h in range(2):
@@ -93,15 +94,24 @@ def tile_picked_gatehead_none_p_kernel(tc, x_words, x_scales, w1, a1, a2, a3, w2
             nc.scalar.copy(w1_b[:, :, 64 * h : 64 * (h + 1), :].rearrange("p t m j -> p m j t"),
                  w1_raw[h][:].rearrange("p j (m t) -> p m j t", t=PACK))
         w1_q = quantize("w1", w1_b[:].rearrange("p t m j -> p (t m j)"), H)
-        xq_w = pick("xq_w", xw, offs_t, U32)
+        xq_w = sb("xq_w", [P, S], U32)
+        for h in range(2):
+            nc.vector.tensor_copy(xq_w[:, h * HALF : (h + 1) * HALF], xw[:].indirect(offs_t[:, h * HALF // GROUP : (h + 1) * HALF // GROUP]))
         xo_s = pick("xo_s", xs, own_t, U8)
         xo_w = pick("xo_w", xw, own_t, U32)
         y = []
         for t in range(PACK):
-            acc = bank("A%d" % t, "y_ps%d" % t, [P, S])
-            mx(acc[:], w1_q, slice(P * t, P * (t + 1)), xq_w[:], xq_s[:])
             y_t = sb("y%d" % t, [P, S], F32)
-            nc.scalar.copy(y_t[:], acc[:])
+            if t == 0:
+                for h, tag in enumerate(("B0", "A0")):
+                    cols = slice(h * HALF, (h + 1) * HALF)
+                    acc = bank(tag, "y_ps0_%d" % h, [P, HALF])
+                    mx(acc[:], w1_q, slice(0, P), xq_w[:, cols], xq_s[:, cols])
+                    nc.scalar.copy(y_t[:, cols], acc[:])
+            else:
+                acc = bank("A%d" % t, "y_ps%d" % t, [P, S])
+                mx(acc[:], w1_q, slice(P * t, P * (t + 1)), xq_w[:], xq_s[:])
+                nc.scalar.copy(y_t[:], acc[:])
             y.append(y_t)
 
         def round_weights(name, raw):
@@ -128,7 +138,7 @@ def tile_picked_gatehead_none_p_kernel(tc, x_words, x_scales, w1, a1, a2, a3, w2
             z_t = [bank("B%d" % b, "zT%d" % b, [P, PACK, P]) for b in blocks]
             for t in range(PACK):
                 for l in range(3):
-                    prod = prods(t)[:, l, :]
+                    prod = prods(t, l)
                     nc.vector.tensor_tensor(prod, y[t][:].indirect(lists[l][:, v0 // GROUP : v1 // GROUP]), gains[l][:, v0:v1], MULT)
                     for i in range(len(blocks)):
                         nc.tensor.matmul(z_t[i][:, t, :], lhsT=prod[:, i * BLK : (i + 1) * BLK], rhs=ident[:],
@@ -137,47 +147,52 @@ def tile_picked_gatehead_none_p_kernel(tc, x_words, x_scales, w1, a1, a2, a3, w2
                     after_pair(t // 2, z_t[0])
             return z_t
 
-        def project(b, zb):
+        def project(b, zb, banks):
             back = bank("A%d" % b, "back%d" % b, [P, 2, BLK])
             for u in range(2):
                 nc.tensor.transpose(back[:, u, :], zb[u].rearrange("v p e -> v (p e)").bitcast(F32), ident[:])
             zq = sb("zq%d" % b, [P, BLK * PACK], BF16)
             nc.scalar.copy(zq[:].bitcast(F32).rearrange("p (v u) -> p v u", u=2), back[:].rearrange("p u v -> p v u"))
             z_q = quantize("z%d" % b, zq[:], BLK)
-            acc = bank("A%d" % b, "o_ps%d" % b, [P, PACK, BLK])
-            for mt in range(PACK):
-                mx(acc[:, mt, :], w2_q, slice(P * mt, P * (mt + 1)), z_q[0][:], z_q[1][:])
-            return acc
+            parts = []
+            for tag, tiles in banks:
+                acc = bank(tag, "o_ps%d_%s" % (b, tag), [P, len(tiles), BLK])
+                for i, mt in enumerate(tiles):
+                    mx(acc[:, i, :], w2_q, slice(P * mt, P * (mt + 1)), z_q[0][:], z_q[1][:])
+                parts.append((acc, tiles))
+            return parts
 
-        def finish(b, acc, tag=None):
-            res = sb("res%d" % b, [P, PACK, BLK], F32, tag)
-            nc.vector.tensor_tensor(res[:], acc[:], gate[:, :, b * BLK : (b + 1) * BLK], MULT)
-            nc.sync.dma_start(out_rows[:, :, b * BLK : (b + 1) * BLK], res[:])
+        def finish(b, parts, tag=None):
+            for acc, tiles in parts:
+                rows = slice(tiles.start, tiles.stop)
+                res = sb("res%d_%d" % (b, tiles.start), [P, len(tiles), BLK], F32, tag)
+                nc.vector.tensor_tensor(res[:], acc[:], gate[:, rows, b * BLK : (b + 1) * BLK], MULT)
+                nc.sync.dma_start(out_rows[:, rows, b * BLK : (b + 1) * BLK], res[:])
 
         make_gate()
         made = {}
 
-        def first_prods(t):
+        def first_prods(t, l):
             if t not in made:
                 made[t] = sb("g%d" % t, [P, 3, 3 * BLK], F32, {2: "w3_b", 3: "w2_b"}.get(t))
-            return made[t]
+            return made[t][:, l, :]
 
         projected = []
         for b, z_b in enumerate(gather_sum([0, 1, 2], first_prods)):
             zb = sb("zb%d" % b, [P, 2, P, 2], BF16)
             nc.scalar.copy(zb[:], z_b[:].rearrange("v (u e) p -> v u p e", e=2))
-            projected.append(project(b, [zb[:, u, :, :] for u in range(2)]))
+            projected.append(project(b, [zb[:, u, :, :] for u in range(2)], [("A%d" % b, range(PACK))]))
 
-        c01 = sb("c01", [P, 2, 3, BLK], F32, "w3_b")
-        c2 = sb("c2", [P, 3, BLK], F32, "zq0")
-        c3 = sb("c3", [P, 3, BLK], F32, "zq1")
-        last_prods = [c01[:, 0, :, :], c01[:, 1, :, :], c2[:], c3[:]]
+        last_prods = []
+        for count, tag in ((8, "w3_b"), (3, "zq0"), (1, "zq1")):
+            c = sb("c_" + tag, [P, count, BLK], F32, tag)
+            last_prods.extend(c[:, i, :] for i in range(count))
         halves = [sb("zb3_%d" % u, [P, P, 2], BF16) for u in range(2)]
 
         def round_pair(u, z_b):
             nc.scalar.copy(halves[u][:], z_b[:, 2 * u : 2 * u + 2, :].rearrange("v e p -> v p e"))
 
-        gather_sum([3], lambda t: last_prods[t], round_pair)
-        projected.append(project(3, [h[:] for h in halves]))
+        gather_sum([3], lambda t, l: last_prods[3 * t + l], round_pair)
+        projected.append(project(3, [h[:] for h in halves], [("B0", range(0, 2)), ("B1", range(2, 4))]))
         for b in range(V // BLK):
-            finish(b, projected[b], "zq0" if b == 0 else None)
+            finish(b, projected[b], {0: "zq0", 2: "zq3"}.get(b))

@@ -44,7 +44,7 @@ def tile_picked_gatehead_none_p_kernel(tc, x_words, x_scales, w1, a1, a2, a3, w2
         offs_t = load_list("offs_t", offs)
         xs_in = sb("xs_in", [P, T], U8)
         for q in range(4):
-            nc.sync.dma_start(xs_in[32 * q : 32 * q + 4, :].bitcast(I32), x_scales[0, 4 * q : 4 * q + 4, :].bitcast(I32))
+            nc.sync.dma_start(xs_in[q:P:32, :].bitcast(I32), x_scales[0, q:16:4, :].bitcast(I32))
         w1_rows = w1.rearrange("(p j) c -> p j c", j=PACK)
         w1_raw = []
         for h in range(2):
@@ -184,7 +184,7 @@ def tile_picked_gatehead_none_p_kernel(tc, x_words, x_scales, w1, a1, a2, a3, w2
             projected.append(project(b, [zb[:, u, :, :] for u in range(2)], [("A%d" % b, range(PACK))]))
 
         last_prods = []
-        for count, tag in ((8, "w3_b"), (3, "zq0"), (1, "zq1")):
+        for count, tag in ((10, "w3_b"), (2, "zq0")):
             c = sb("c_" + tag, [P, count, BLK], F32, tag)
             last_prods.extend(c[:, i, :] for i in range(count))
         halves = [sb("zb3_%d" % u, [P, P, 2], BF16) for u in range(2)]
@@ -195,4 +195,4 @@ def tile_picked_gatehead_none_p_kernel(tc, x_words, x_scales, w1, a1, a2, a3, w2
         gather_sum([3], lambda t, l: last_prods[3 * t + l], round_pair)
         projected.append(project(3, [h[:] for h in halves], [("B0", range(0, 2)), ("B1", range(2, 4))]))
         for b in range(V // BLK):
-            finish(b, projected[b], {0: "zq0", 2: "zq3"}.get(b))
+            finish(b, projected[b], "zq0" if b == 0 else None)

from contextlib import ExitStack

import concourse.mybir as mybir
from concourse.masks import make_identity

K, T, S, V, H, N = 512, 2048, 512, 512, 512, 512
FLOPS = 2 * K * H * S + 2 * H * N * V + 2 * K * N * V
BYTES = K * T + 16 * T + 4 * (K * H + H * N + K * N) + 3 * 4 * 8 * V + 5 * 2 * 128 * 32 + 4 * N * V

F32 = mybir.dt.float32
BF16 = mybir.dt.bfloat16
I32 = mybir.dt.int32
U32 = mybir.dt.uint32
U16 = mybir.dt.uint16
U8 = mybir.dt.uint8
FP8X4 = mybir.dt.float8_e4m3fn_x4
MULT = mybir.AluOpType.mult
SIGMOID = mybir.ActivationFunctionType.Sigmoid

P = 128
PACK = 4
GROUP = 16
BLK = 128
HALF = 256


def tile_picked_gatehead_none_p_kernel(tc, x_words, x_scales, w1, a1, a2, a3, w2, w3, offs, p1, p2, p3, own, out):
    nc = tc.nc
    with ExitStack() as ctx:
        keep = ctx.enter_context(tc.tile_pool(name="keep", bufs=1))
        psum = ctx.enter_context(tc.psum_pool(name="psum", bufs=1))

        def sb(name, shape, dtype, tag=None):
            return keep.tile(shape, dtype, name=name, tag=tag or name, align_bytes=64)

        def bank(tag, name, shape):
            return psum.tile(shape, F32, name=name, tag=tag)

        def load_list(name, src):
            t = keep.tile([P, S // GROUP], U16, name=name)
            nc.sync.dma_start(t[:], src)
            return t

        offs_t = load_list("offs_t", offs)
        xs_in = sb("xs_in", [P, T], U8)
        for q in range(4):
            nc.sync.dma_start(xs_in[q:P:32, :].bitcast(I32), x_scales[0, q:16:4, :].bitcast(I32))
        w1_rows = w1.rearrange("(p j) c -> p j c", j=PACK)
        w1_raw = []
        for h in range(2):
            t = sb("w1_raw%d" % h, [P, PACK, H // 2], F32)
            nc.sync.dma_start(t[:], w1_rows[:, :, h * (H // 2) : (h + 1) * (H // 2)])
            w1_raw.append(t)
        own_t = load_list("own_t", own)
        xw = sb("xw", [P, T], U32)
        nc.sync.dma_start(xw[:].bitcast(I32), x_words[0].rearrange("p n j -> p (n j)").bitcast(I32))
        lists, gains = [], []
        for l, (p_l, a_l) in enumerate(((p1, a1), (p2, a2), (p3, a3))):
            lists.append(load_list("p%d_t" % l, p_l))
            g = sb("a%d_t" % l, [P, V], F32)
            nc.sync.dma_start(g[:], a_l.rearrange("(p j) v -> p j v", j=PACK)[:, 0, :])
            gains.append(g)
        w3_raw = sb("w3_raw", [P, PACK, N], F32)
        nc.sync.dma_start(w3_raw[:], w3.rearrange("(p j) c -> p j c", j=PACK))
        w2_raw = sb("w2_raw", [P, PACK, N], F32)
        nc.sync.dma_start(w2_raw[:], w2.rearrange("(p j) c -> p j c", j=PACK))

        ident = sb("ident", [P, P], F32)
        make_identity(nc, ident[:])

        def pick(name, table, lst, dtype):
            t = sb(name, [P, S], dtype)
            nc.vector.tensor_copy(t[:], table[:].indirect(lst[:]))
            return t

        xs = sb("xs", [P, T], U8)
        nc.vector.memset(xs[:].bitcast(I32), 0)
        for q in range(4):
            nc.vector.tensor_copy(xs[32 * q : 32 * q + 4, :].bitcast(I32), xs_in[32 * q : 32 * q + 4, :].bitcast(I32))
        xq_s = pick("xq_s", xs, offs_t, U8)

        def quantize(name, grouped, width):
            codes = sb(name + "_codes", [P, width], U32)
            scales = sb(name + "_scales", [P, width], U8)
            nc.vector.quantize_mx(out=codes[:].bitcast(FP8X4), scales=scales[:], in_=grouped)
            return codes, scales

        def mx(out_ap, w_q, cols, x_codes, x_scale):
            nc.tensor.matmul_mx(out=out_ap, lhsT=w_q[0][:, cols].bitcast(FP8X4), lhsT_scale=w_q[1][:, cols],
                                rhs=x_codes.bitcast(FP8X4), rhs_scale=x_scale, start=True, stop=True)

        w1_b = sb("w1_b", [P, PACK, P, PACK], BF16)
        for h in range(2):
            nc.scalar.copy(w1_b[:, :, 64 * h : 64 * (h + 1), :].rearrange("p t m j -> p m j t"),
                 w1_raw[h][:].rearrange("p j (m t) -> p m j t", t=PACK))
        w1_q = quantize("w1", w1_b[:].rearrange("p t m j -> p (t m j)"), H)
        xq_w = sb("xq_w", [P, S], U32)
        for h in range(2):
            nc.vector.tensor_copy(xq_w[:, h * HALF : (h + 1) * HALF], xw[:].indirect(offs_t[:, h * HALF // GROUP : (h + 1) * HALF // GROUP]))
        xo_s = pick("xo_s", xs, own_t, U8)
        xo_w = pick("xo_w", xw, own_t, U32)
        y = []
        for t in range(PACK):
            y_t = sb("y%d" % t, [P, S], F32)
            if t == 0:
                for h, tag in enumerate(("B0", "A0")):
                    cols = slice(h * HALF, (h + 1) * HALF)
                    acc = bank(tag, "y_ps0_%d" % h, [P, HALF])
                    mx(acc[:], w1_q, slice(0, P), xq_w[:, cols], xq_s[:, cols])
                    nc.scalar.copy(y_t[:, cols], acc[:])
            else:
                acc = bank("A%d" % t, "y_ps%d" % t, [P, S])
                mx(acc[:], w1_q, slice(P * t, P * (t + 1)), xq_w[:], xq_s[:])
                nc.scalar.copy(y_t[:], acc[:])
            y.append(y_t)

        def round_weights(name, raw):
            grouped = sb(name, [P, N, PACK], BF16)
            nc.scalar.copy(grouped[:].rearrange("p (c i) j -> p c j i", i=4), raw[:].rearrange("p j (c i) -> p c j i", i=4))
            return grouped[:].rearrange("p c j -> p (c j)")

        w3_q = quantize("w3", round_weights("w3_b", w3_raw), N)
        w2_b = round_weights("w2_b", w2_raw)
        w2_q = quantize("w2", w2_b, N)

        gate = sb("gate", [P, PACK, V], F32)

        def make_gate():
            for mt in range(PACK):
                acc = bank("A%d" % mt, "g_ps%d" % mt, [P, V])
                mx(acc[:], w3_q, slice(P * mt, P * (mt + 1)), xo_w[:], xo_s[:])
                nc.scalar.activation(gate[:, mt, :], acc[:], SIGMOID)

        out_rows = out.rearrange("(mt p) v -> p mt v", p=P)

        def gather_sum(blocks, prods, after_pair=None):
            v0, v1 = blocks[0] * BLK, (blocks[-1] + 1) * BLK
            z_t = [bank("B%d" % b, "zT%d" % b, [P, PACK, P]) for b in blocks]
            for t in range(PACK):
                for l in range(3):
                    prod = prods(t, l)
                    nc.vector.tensor_tensor(prod, y[t][:].indirect(lists[l][:, v0 // GROUP : v1 // GROUP]), gains[l][:, v0:v1], MULT)
                    for i in range(len(blocks)):
                        nc.tensor.matmul(z_t[i][:, t, :], lhsT=prod[:, i * BLK : (i + 1) * BLK], rhs=ident[:],
                                         is_transpose=True, start=(l == 0), stop=(l == 2))
                if after_pair is not None and t % 2 == 1:
                    after_pair(t // 2, z_t[0])
            return z_t

        def project(b, zb, banks):
            back = bank("A%d" % b, "back%d" % b, [P, 2, BLK])
            for u in range(2):
                nc.tensor.transpose(back[:, u, :], zb[u].rearrange("v p e -> v (p e)").bitcast(F32), ident[:])
            zq = sb("zq%d" % b, [P, BLK * PACK], BF16)
            nc.scalar.copy(zq[:].bitcast(F32).rearrange("p (v u) -> p v u", u=2), back[:].rearrange("p u v -> p v u"))
            z_q = quantize("z%d" % b, zq[:], BLK)
            parts = []
            for tag, tiles in banks:
                acc = bank(tag, "o_ps%d_%s" % (b, tag), [P, len(tiles), BLK])
                for i, mt in enumerate(tiles):
                    mx(acc[:, i, :], w2_q, slice(P * mt, P * (mt + 1)), z_q[0][:], z_q[1][:])
                parts.append((acc, tiles))
            return parts

        def finish(b, parts, tag=None):
            for acc, tiles in parts:
                rows = slice(tiles.start, tiles.stop)
                res = sb("res%d_%d" % (b, tiles.start), [P, len(tiles), BLK], F32, tag)
                nc.vector.tensor_tensor(res[:], acc[:], gate[:, rows, b * BLK : (b + 1) * BLK], MULT)
                nc.sync.dma_start(out_rows[:, rows, b * BLK : (b + 1) * BLK], res[:])

        make_gate()
        made = {}

        def first_prods(t, l):
            if t not in made:
                made[t] = sb("g%d" % t, [P, 3, 3 * BLK], F32, {2: "w3_b", 3: "w2_b"}.get(t))
            return made[t][:, l, :]

        projected = []
        for b, z_b in enumerate(gather_sum([0, 1, 2], first_prods)):
            zb = sb("zb%d" % b, [P, 2, P, 2], BF16)
            nc.scalar.copy(zb[:], z_b[:].rearrange("v (u e) p -> v u p e", e=2))
            projected.append(project(b, [zb[:, u, :, :] for u in range(2)], [("A%d" % b, range(PACK))]))

        last_prods = []
        for count, tag in ((10, "w3_b"), (2, "zq0")):
            c = sb("c_" + tag, [P, count, BLK], F32, tag)
            last_prods.extend(c[:, i, :] for i in range(count))
        halves = [sb("zb3_%d" % u, [P, P, 2], BF16) for u in range(2)]

        def round_pair(u, z_b):
            nc.scalar.copy(halves[u][:], z_b[:, 2 * u : 2 * u + 2, :].rearrange("v e p -> v p e"))

        gather_sum([3], lambda t, l: last_prods[3 * t + l], round_pair)
        projected.append(project(3, [h[:] for h in halves], [("B0", range(0, 2)), ("B1", range(2, 4))]))
        for b in range(V // BLK):
            finish(b, projected[b], "zq0" if b == 0 else None)
